import numpy as np
import ml_dtypes

BF16 = ml_dtypes.bfloat16


def bf(x):
    return np.asarray(x, np.float32).astype(BF16)


def f32(x):
    return np.asarray(x, np.float32)


def f64(x):
    return np.asarray(x).astype(np.float64)


def striped(idx):
    return np.concatenate([l.reshape(-1, 16).T for l in idx])


def rows(idx, k):
    return np.tile(np.repeat(idx, 16, axis=0), (k // (16 * 8), 1))


def look(tab, idx):
    return np.take_along_axis(f64(tab), rows(idx, len(tab)), axis=1)


K, S, V, N = 128, 2048, 2048, 2048


def silu(v):
    return v / (1.0 + np.exp(-v))


def setup_inputs():
    return {"tab": f32(np.random.standard_normal((2, K, S))), "y": f32(np.random.standard_normal((K, V))), "offs": striped(np.stack([np.random.permutation(S)[:N] for _ in range(8)]))}


def reference(tab, y, offs):
    idx = np.stack([g.T.reshape(-1) for g in np.split(offs, 8)])
    x = (look(tab[0], idx) - f64(y)) * (silu(look(tab[1], idx)))
    return x

@@ -1,0 +1,32 @@
+import concourse.mybir as mybir
+
+F32 = mybir.dt.float32
+U16 = mybir.dt.uint16
+GROUP = 16
+PIECE = 512
+
+
+def tile_lookup_vg_subsilu_out_kernel(tc, tab, y, offs, out):
+    nc = tc.nc
+    rows, places = tab.shape[1], tab.shape[2]
+    entries = y.shape[1]
+    pieces = entries // PIECE
+    with tc.tile_pool(name="held", bufs=1) as held, tc.tile_pool(name="work", bufs=pieces) as work:
+        offsets = held.tile([rows, entries // GROUP], U16, name="offsets")
+        values = held.tile([rows, places], F32, name="values")
+        gates = held.tile([rows, places], F32, name="gates")
+        stream = held.tile([rows, entries], F32, name="stream")
+        nc.sync.dma_start(offsets[:], offs)
+        nc.sync.dma_start(values[:], tab[0])
+        nc.sync.dma_start(gates[:], tab[1])
+        nc.sync.dma_start(stream[:], y)
+        for piece in range(pieces):
+            columns = slice(piece * PIECE, (piece + 1) * PIECE)
+            picks = offsets[:, piece * PIECE // GROUP : (piece + 1) * PIECE // GROUP]
+            difference = work.tile([rows, PIECE], F32, name="difference")
+            gate = work.tile([rows, PIECE], F32, name="gate")
+            product = work.tile([rows, PIECE], F32, name="product")
+            nc.vector.tensor_tensor(difference[:], values[:].indirect(picks), stream[:, columns], mybir.AluOpType.subtract)
+            nc.scalar.activation(gate[:], gates[:].indirect(picks), mybir.ActivationFunctionType.Silu)
+            nc.vector.tensor_tensor(product[:], difference[:], gate[:], mybir.AluOpType.mult)
+            nc.sync.dma_start(out[:, columns], product[:])

@@ -2,6 +2,7 @@ import concourse.mybir as mybir
 
 F32 = mybir.dt.float32
 U16 = mybir.dt.uint16
+SILU = mybir.ActivationFunctionType.Silu
 GROUP = 16
 PIECE = 512
 
@@ -15,18 +16,28 @@ def tile_lookup_vg_subsilu_out_kernel(tc, tab, y, offs, out):
         offsets = held.tile([rows, entries // GROUP], U16, name="offsets")
         values = held.tile([rows, places], F32, name="values")
         gates = held.tile([rows, places], F32, name="gates")
-        stream = held.tile([rows, entries], F32, name="stream")
+        streams = [work.tile([rows, PIECE], F32, name="stream") for piece in range(pieces)]
+        columns = [slice(piece * PIECE, (piece + 1) * PIECE) for piece in range(pieces)]
+
+        zeros = held.tile([rows, 1], F32, name="zeros")
+        warm = held.tile([rows, 1], F32, name="warm")
+        nc.vector.memset(zeros[:], 0.0)
+        nc.scalar.activation(warm[:], zeros[:], SILU)
+
         nc.sync.dma_start(offsets[:], offs)
         nc.sync.dma_start(values[:], tab[0])
+        for piece in range(pieces // 2):
+            nc.sync.dma_start(streams[piece][:], y[:, columns[piece]])
         nc.sync.dma_start(gates[:], tab[1])
-        nc.sync.dma_start(stream[:], y)
+        for piece in range(pieces // 2, pieces):
+            nc.sync.dma_start(streams[piece][:], y[:, columns[piece]])
+
         for piece in range(pieces):
-            columns = slice(piece * PIECE, (piece + 1) * PIECE)
             picks = offsets[:, piece * PIECE // GROUP : (piece + 1) * PIECE // GROUP]
             difference = work.tile([rows, PIECE], F32, name="difference")
             gate = work.tile([rows, PIECE], F32, name="gate")
             product = work.tile([rows, PIECE], F32, name="product")
-            nc.vector.tensor_tensor(difference[:], values[:].indirect(picks), stream[:, columns], mybir.AluOpType.subtract)
-            nc.scalar.activation(gate[:], gates[:].indirect(picks), mybir.ActivationFunctionType.Silu)
+            nc.vector.tensor_tensor(difference[:], values[:].indirect(picks), streams[piece][:], mybir.AluOpType.subtract)
+            nc.scalar.activation(gate[:], gates[:].indirect(picks), SILU)
             nc.vector.tensor_tensor(product[:], difference[:], gate[:], mybir.AluOpType.mult)
-            nc.sync.dma_start(out[:, columns], product[:])
+            nc.sync.dma_start(out[:, columns[piece]], product[:])

@@ -11,33 +11,35 @@ def tile_lookup_vg_subsilu_out_kernel(tc, tab, y, offs, out):
     nc = tc.nc
     rows, places = tab.shape[1], tab.shape[2]
     entries = y.shape[1]
-    pieces = entries // PIECE
-    with tc.tile_pool(name="held", bufs=1) as held, tc.tile_pool(name="work", bufs=pieces) as work:
+    with tc.tile_pool(name="held", bufs=1) as held:
         offsets = held.tile([rows, entries // GROUP], U16, name="offsets")
         values = held.tile([rows, places], F32, name="values")
         gates = held.tile([rows, places], F32, name="gates")
-        streams = [work.tile([rows, PIECE], F32, name="stream") for piece in range(pieces)]
-        columns = [slice(piece * PIECE, (piece + 1) * PIECE) for piece in range(pieces)]
+        stream = held.tile([rows, entries], F32, name="stream")
+        difference = held.tile([rows, entries], F32, name="difference")
+        silu = held.tile([rows, entries], F32, name="silu")
+        product = held.tile([rows, entries], F32, name="product")
 
         zeros = held.tile([rows, 1], F32, name="zeros")
         warm = held.tile([rows, 1], F32, name="warm")
         nc.vector.memset(zeros[:], 0.0)
         nc.scalar.activation(warm[:], zeros[:], SILU)
 
+        early = entries // 2
         nc.sync.dma_start(offsets[:], offs)
         nc.sync.dma_start(values[:], tab[0])
-        for piece in range(pieces // 2):
-            nc.sync.dma_start(streams[piece][:], y[:, columns[piece]])
+        nc.sync.dma_start(stream[:, :early], y[:, :early])
         nc.sync.dma_start(gates[:], tab[1])
-        for piece in range(pieces // 2, pieces):
-            nc.sync.dma_start(streams[piece][:], y[:, columns[piece]])
+        for start in range(early, entries, PIECE):
+            nc.sync.dma_start(stream[:, start : start + PIECE], y[:, start : start + PIECE])
 
-        for piece in range(pieces):
-            picks = offsets[:, piece * PIECE // GROUP : (piece + 1) * PIECE // GROUP]
-            difference = work.tile([rows, PIECE], F32, name="difference")
-            gate = work.tile([rows, PIECE], F32, name="gate")
-            product = work.tile([rows, PIECE], F32, name="product")
-            nc.vector.tensor_tensor(difference[:], values[:].indirect(picks), streams[piece][:], mybir.AluOpType.subtract)
-            nc.scalar.activation(gate[:], gates[:].indirect(picks), SILU)
-            nc.vector.tensor_tensor(product[:], difference[:], gate[:], mybir.AluOpType.mult)
-            nc.sync.dma_start(out[:, columns[piece]], product[:])
+        for start in range(0, entries, PIECE):
+            picks = offsets[:, start // GROUP : (start + PIECE) // GROUP]
+            columns = slice(start, start + PIECE)
+            nc.vector.tensor_tensor(difference[:, columns], values[:].indirect(picks), stream[:, columns], mybir.AluOpType.subtract)
+            nc.scalar.activation(silu[:, columns], gates[:].indirect(picks), SILU)
+
+        cuts = list(range(0, entries, PIECE)) + [entries - PIECE // 2, entries]
+        for start, stop in zip(cuts, cuts[1:]):
+            nc.vector.tensor_tensor(product[:, start:stop], difference[:, start:stop], silu[:, start:stop], mybir.AluOpType.mult)
+            nc.sync.dma_start(out[:, start:stop], product[:, start:stop])

@@ -28,18 +28,29 @@ def tile_lookup_vg_subsilu_out_kernel(tc, tab, y, offs, out):
         early = entries // 2
         nc.sync.dma_start(offsets[:], offs)
         nc.sync.dma_start(values[:], tab[0])
-        nc.sync.dma_start(stream[:, :early], y[:, :early])
+        nc.scalar.dma_start(stream[:, :early], y[:, :early])
         nc.sync.dma_start(gates[:], tab[1])
         for start in range(early, entries, PIECE):
             nc.sync.dma_start(stream[:, start : start + PIECE], y[:, start : start + PIECE])
 
-        for start in range(0, entries, PIECE):
+        def subtract(start):
             picks = offsets[:, start // GROUP : (start + PIECE) // GROUP]
             columns = slice(start, start + PIECE)
             nc.vector.tensor_tensor(difference[:, columns], values[:].indirect(picks), stream[:, columns], mybir.AluOpType.subtract)
-            nc.scalar.activation(silu[:, columns], gates[:].indirect(picks), SILU)
 
-        cuts = list(range(0, entries, PIECE)) + [entries - PIECE // 2, entries]
-        for start, stop in zip(cuts, cuts[1:]):
+        def multiply_and_store(start, stop):
             nc.vector.tensor_tensor(product[:, start:stop], difference[:, start:stop], silu[:, start:stop], mybir.AluOpType.mult)
             nc.sync.dma_start(out[:, start:stop], product[:, start:stop])
+
+        for start in range(0, entries, PIECE):
+            picks = offsets[:, start // GROUP : (start + PIECE) // GROUP]
+            nc.scalar.activation(silu[:, start : start + PIECE], gates[:].indirect(picks), SILU)
+
+        last = entries - PIECE
+        for start in range(0, last, PIECE):
+            subtract(start)
+        multiply_and_store(0, PIECE)
+        subtract(last)
+        cuts = list(range(PIECE, entries, PIECE)) + [entries - PIECE // 2, entries]
+        for start, stop in zip(cuts, cuts[1:]):
+            multiply_and_store(start, stop)

@@ -5,6 +5,7 @@ U16 = mybir.dt.uint16
 SILU = mybir.ActivationFunctionType.Silu
 GROUP = 16
 PIECE = 512
+EARLY = 768
 
 
 def tile_lookup_vg_subsilu_out_kernel(tc, tab, y, offs, out):
@@ -25,18 +26,17 @@ def tile_lookup_vg_subsilu_out_kernel(tc, tab, y, offs, out):
         nc.vector.memset(zeros[:], 0.0)
         nc.scalar.activation(warm[:], zeros[:], SILU)
 
-        early = entries // 2
+        middle = EARLY + PIECE
         nc.sync.dma_start(offsets[:], offs)
         nc.sync.dma_start(values[:], tab[0])
-        nc.scalar.dma_start(stream[:, :early], y[:, :early])
+        nc.scalar.dma_start(stream[:, :EARLY], y[:, :EARLY])
         nc.sync.dma_start(gates[:], tab[1])
-        for start in range(early, entries, PIECE):
-            nc.sync.dma_start(stream[:, start : start + PIECE], y[:, start : start + PIECE])
+        nc.sync.dma_start(stream[:, EARLY:middle], y[:, EARLY:middle])
+        nc.sync.dma_start(stream[:, middle:], y[:, middle:])
 
-        def subtract(start):
-            picks = offsets[:, start // GROUP : (start + PIECE) // GROUP]
-            columns = slice(start, start + PIECE)
-            nc.vector.tensor_tensor(difference[:, columns], values[:].indirect(picks), stream[:, columns], mybir.AluOpType.subtract)
+        def subtract(start, stop):
+            picks = offsets[:, start // GROUP : stop // GROUP]
+            nc.vector.tensor_tensor(difference[:, start:stop], values[:].indirect(picks), stream[:, start:stop], mybir.AluOpType.subtract)
 
         def multiply_and_store(start, stop):
             nc.vector.tensor_tensor(product[:, start:stop], difference[:, start:stop], silu[:, start:stop], mybir.AluOpType.mult)
@@ -46,11 +46,9 @@ def tile_lookup_vg_subsilu_out_kernel(tc, tab, y, offs, out):
             picks = offsets[:, start // GROUP : (start + PIECE) // GROUP]
             nc.scalar.activation(silu[:, start : start + PIECE], gates[:].indirect(picks), SILU)
 
-        last = entries - PIECE
-        for start in range(0, last, PIECE):
-            subtract(start)
+        subtract(0, EARLY)
+        subtract(EARLY, middle)
         multiply_and_store(0, PIECE)
-        subtract(last)
-        cuts = list(range(PIECE, entries, PIECE)) + [entries - PIECE // 2, entries]
-        for start, stop in zip(cuts, cuts[1:]):
-            multiply_and_store(start, stop)
+        subtract(middle, entries)
+        for start in range(PIECE, entries, PIECE // 2):
+            multiply_and_store(start, start + PIECE // 2)

@@ -5,7 +5,7 @@ U16 = mybir.dt.uint16
 SILU = mybir.ActivationFunctionType.Silu
 GROUP = 16
 PIECE = 512
-EARLY = 768
+EARLY = 832
 
 
 def tile_lookup_vg_subsilu_out_kernel(tc, tab, y, offs, out):
@@ -42,13 +42,14 @@ def tile_lookup_vg_subsilu_out_kernel(tc, tab, y, offs, out):
             nc.vector.tensor_tensor(product[:, start:stop], difference[:, start:stop], silu[:, start:stop], mybir.AluOpType.mult)
             nc.sync.dma_start(out[:, start:stop], product[:, start:stop])
 
-        for start in range(0, entries, PIECE):
-            picks = offsets[:, start // GROUP : (start + PIECE) // GROUP]
-            nc.scalar.activation(silu[:, start : start + PIECE], gates[:].indirect(picks), SILU)
+        for start, stop in ((0, PIECE), (PIECE, entries - PIECE), (entries - PIECE, entries)):
+            nc.scalar.activation(silu[:, start:stop], gates[:].indirect(offsets[:, start // GROUP : stop // GROUP]), SILU)
 
         subtract(0, EARLY)
         subtract(EARLY, middle)
-        multiply_and_store(0, PIECE)
+        nc.vector.tensor_tensor(product[:, :PIECE], difference[:, :PIECE], silu[:, :PIECE], mybir.AluOpType.mult)
+        for start in range(0, PIECE, PIECE // 4):
+            nc.sync.dma_start(out[:, start : start + PIECE // 4], product[:, start : start + PIECE // 4])
         subtract(middle, entries)
         for start in range(PIECE, entries, PIECE // 2):
             multiply_and_store(start, start + PIECE // 2)

@@ -40,7 +40,7 @@ def tile_lookup_vg_subsilu_out_kernel(tc, tab, y, offs, out):
 
         def multiply_and_store(start, stop):
             nc.vector.tensor_tensor(product[:, start:stop], difference[:, start:stop], silu[:, start:stop], mybir.AluOpType.mult)
-            nc.sync.dma_start(out[:, start:stop], product[:, start:stop])
+            nc.scalar.dma_start(out[:, start:stop], product[:, start:stop])
 
         for start, stop in ((0, PIECE), (PIECE, entries - PIECE), (entries - PIECE, entries)):
             nc.scalar.activation(silu[:, start:stop], gates[:].indirect(offsets[:, start // GROUP : stop // GROUP]), SILU)
@@ -49,7 +49,7 @@ def tile_lookup_vg_subsilu_out_kernel(tc, tab, y, offs, out):
         subtract(EARLY, middle)
         nc.vector.tensor_tensor(product[:, :PIECE], difference[:, :PIECE], silu[:, :PIECE], mybir.AluOpType.mult)
         for start in range(0, PIECE, PIECE // 4):
-            nc.sync.dma_start(out[:, start : start + PIECE // 4], product[:, start : start + PIECE // 4])
+            nc.scalar.dma_start(out[:, start : start + PIECE // 4], product[:, start : start + PIECE // 4])
         subtract(middle, entries)
         for start in range(PIECE, entries, PIECE // 2):
             multiply_and_store(start, start + PIECE // 2)

@@ -3,15 +3,26 @@ import concourse.mybir as mybir
 F32 = mybir.dt.float32
 U16 = mybir.dt.uint16
 SILU = mybir.ActivationFunctionType.Silu
+SUBTRACT = mybir.AluOpType.subtract
+MULT = mybir.AluOpType.mult
 GROUP = 16
-PIECE = 512
+LAST = 512
 EARLY = 832
+FIRST = 640
+STEP = 64
+
+
+def rising(start, stop, count):
+    width = (stop - start - STEP * count * (count - 1) // 2) // count
+    edges = [start + k * width + STEP * k * (k - 1) // 2 for k in range(count)] + [stop]
+    return list(zip(edges, edges[1:]))
 
 
 def tile_lookup_vg_subsilu_out_kernel(tc, tab, y, offs, out):
     nc = tc.nc
     rows, places = tab.shape[1], tab.shape[2]
     entries = y.shape[1]
+    middle = EARLY + LAST
     with tc.tile_pool(name="held", bufs=1) as held:
         offsets = held.tile([rows, entries // GROUP], U16, name="offsets")
         values = held.tile([rows, places], F32, name="values")
@@ -26,7 +37,6 @@ def tile_lookup_vg_subsilu_out_kernel(tc, tab, y, offs, out):
         nc.vector.memset(zeros[:], 0.0)
         nc.scalar.activation(warm[:], zeros[:], SILU)
 
-        middle = EARLY + PIECE
         nc.sync.dma_start(offsets[:], offs)
         nc.sync.dma_start(values[:], tab[0])
         nc.scalar.dma_start(stream[:, :EARLY], y[:, :EARLY])
@@ -36,20 +46,23 @@ def tile_lookup_vg_subsilu_out_kernel(tc, tab, y, offs, out):
 
         def subtract(start, stop):
             picks = offsets[:, start // GROUP : stop // GROUP]
-            nc.vector.tensor_tensor(difference[:, start:stop], values[:].indirect(picks), stream[:, start:stop], mybir.AluOpType.subtract)
+            nc.vector.tensor_tensor(difference[:, start:stop], values[:].indirect(picks), stream[:, start:stop], SUBTRACT)
 
-        def multiply_and_store(start, stop):
-            nc.vector.tensor_tensor(product[:, start:stop], difference[:, start:stop], silu[:, start:stop], mybir.AluOpType.mult)
+        def multiply(start, stop):
+            nc.vector.tensor_tensor(product[:, start:stop], difference[:, start:stop], silu[:, start:stop], MULT)
+
+        def store(start, stop):
             nc.scalar.dma_start(out[:, start:stop], product[:, start:stop])
 
-        for start, stop in ((0, PIECE), (PIECE, entries - PIECE), (entries - PIECE, entries)):
+        for start, stop in ((0, FIRST), (FIRST, entries - LAST), (entries - LAST, entries)):
             nc.scalar.activation(silu[:, start:stop], gates[:].indirect(offsets[:, start // GROUP : stop // GROUP]), SILU)
 
         subtract(0, EARLY)
         subtract(EARLY, middle)
-        nc.vector.tensor_tensor(product[:, :PIECE], difference[:, :PIECE], silu[:, :PIECE], mybir.AluOpType.mult)
-        for start in range(0, PIECE, PIECE // 4):
-            nc.scalar.dma_start(out[:, start : start + PIECE // 4], product[:, start : start + PIECE // 4])
+        multiply(0, FIRST)
+        for start in range(0, FIRST, FIRST // 4):
+            store(start, start + FIRST // 4)
         subtract(middle, entries)
-        for start in range(PIECE, entries, PIECE // 2):
-            multiply_and_store(start, start + PIECE // 2)
+        for start, stop in rising(FIRST, entries - LAST, 4) + [(entries - LAST, entries - LAST // 2), (entries - LAST // 2, entries)]:
+            multiply(start, stop)
+            store(start, stop)

@@ -8,7 +8,7 @@ MULT = mybir.AluOpType.mult
 GROUP = 16
 LAST = 512
 EARLY = 832
-FIRST = 640
+FIRST = 512
 STEP = 64
 
 

@@ -5,17 +5,12 @@ U16 = mybir.dt.uint16
 SILU = mybir.ActivationFunctionType.Silu
 SUBTRACT = mybir.AluOpType.subtract
 MULT = mybir.AluOpType.mult
+ALIGN = 256
 GROUP = 16
 LAST = 512
 EARLY = 832
 FIRST = 512
-STEP = 64
-
-
-def rising(start, stop, count):
-    width = (stop - start - STEP * count * (count - 1) // 2) // count
-    edges = [start + k * width + STEP * k * (k - 1) // 2 for k in range(count)] + [stop]
-    return list(zip(edges, edges[1:]))
+LEAD = 64
 
 
 def tile_lookup_vg_subsilu_out_kernel(tc, tab, y, offs, out):
@@ -24,13 +19,13 @@ def tile_lookup_vg_subsilu_out_kernel(tc, tab, y, offs, out):
     entries = y.shape[1]
     middle = EARLY + LAST
     with tc.tile_pool(name="held", bufs=1) as held:
-        offsets = held.tile([rows, entries // GROUP], U16, name="offsets")
-        values = held.tile([rows, places], F32, name="values")
-        gates = held.tile([rows, places], F32, name="gates")
-        stream = held.tile([rows, entries], F32, name="stream")
-        difference = held.tile([rows, entries], F32, name="difference")
-        silu = held.tile([rows, entries], F32, name="silu")
-        product = held.tile([rows, entries], F32, name="product")
+        offsets = held.tile([rows, entries // GROUP], U16, name="offsets", align_bytes=ALIGN)
+        values = held.tile([rows, places], F32, name="values", align_bytes=ALIGN)
+        gates = held.tile([rows, places], F32, name="gates", align_bytes=ALIGN)
+        stream = held.tile([rows, entries], F32, name="stream", align_bytes=ALIGN)
+        difference = held.tile([rows, entries], F32, name="difference", align_bytes=ALIGN)
+        silu = held.tile([rows, entries], F32, name="silu", align_bytes=ALIGN)
+        product = held.tile([rows, entries], F32, name="product", align_bytes=ALIGN)
 
         zeros = held.tile([rows, 1], F32, name="zeros")
         warm = held.tile([rows, 1], F32, name="warm")
@@ -63,6 +58,9 @@ def tile_lookup_vg_subsilu_out_kernel(tc, tab, y, offs, out):
         for start in range(0, FIRST, FIRST // 4):
             store(start, start + FIRST // 4)
         subtract(middle, entries)
-        for start, stop in rising(FIRST, entries - LAST, 4) + [(entries - LAST, entries - LAST // 2), (entries - LAST // 2, entries)]:
+        half = LAST // 2
+        led = [cut - LEAD for cut in range(FIRST + half, entries - LAST, half)]
+        edges = [FIRST] + led + [entries - LAST, entries - half, entries]
+        for start, stop in zip(edges, edges[1:]):
             multiply(start, stop)
             store(start, stop)

@@ -5,12 +5,11 @@ U16 = mybir.dt.uint16
 SILU = mybir.ActivationFunctionType.Silu
 SUBTRACT = mybir.AluOpType.subtract
 MULT = mybir.AluOpType.mult
-ALIGN = 256
+ALIGN = 4096
 GROUP = 16
 LAST = 512
 EARLY = 832
 FIRST = 512
-LEAD = 64
 
 
 def tile_lookup_vg_subsilu_out_kernel(tc, tab, y, offs, out):
@@ -58,9 +57,6 @@ def tile_lookup_vg_subsilu_out_kernel(tc, tab, y, offs, out):
         for start in range(0, FIRST, FIRST // 4):
             store(start, start + FIRST // 4)
         subtract(middle, entries)
-        half = LAST // 2
-        led = [cut - LEAD for cut in range(FIRST + half, entries - LAST, half)]
-        edges = [FIRST] + led + [entries - LAST, entries - half, entries]
-        for start, stop in zip(edges, edges[1:]):
-            multiply(start, stop)
-            store(start, stop)
+        for start in range(FIRST, entries, LAST // 2):
+            multiply(start, start + LAST // 2)
+            store(start, start + LAST // 2)

@@ -6,6 +6,7 @@ SILU = mybir.ActivationFunctionType.Silu
 SUBTRACT = mybir.AluOpType.subtract
 MULT = mybir.AluOpType.mult
 ALIGN = 4096
+APART = 32768
 GROUP = 16
 LAST = 512
 EARLY = 832
@@ -18,16 +19,16 @@ def tile_lookup_vg_subsilu_out_kernel(tc, tab, y, offs, out):
     entries = y.shape[1]
     middle = EARLY + LAST
     with tc.tile_pool(name="held", bufs=1) as held:
-        offsets = held.tile([rows, entries // GROUP], U16, name="offsets", align_bytes=ALIGN)
-        values = held.tile([rows, places], F32, name="values", align_bytes=ALIGN)
-        gates = held.tile([rows, places], F32, name="gates", align_bytes=ALIGN)
-        stream = held.tile([rows, entries], F32, name="stream", align_bytes=ALIGN)
-        difference = held.tile([rows, entries], F32, name="difference", align_bytes=ALIGN)
-        silu = held.tile([rows, entries], F32, name="silu", align_bytes=ALIGN)
-        product = held.tile([rows, entries], F32, name="product", align_bytes=ALIGN)
+        offsets = held.tile([rows, entries // GROUP], U16, name="offsets", align_bytes=ALIGN, offset=0 * APART)
+        values = held.tile([rows, places], F32, name="values", align_bytes=ALIGN, offset=1 * APART)
+        gates = held.tile([rows, places], F32, name="gates", align_bytes=ALIGN, offset=2 * APART)
+        stream = held.tile([rows, entries], F32, name="stream", align_bytes=ALIGN, offset=3 * APART)
+        difference = held.tile([rows, entries], F32, name="difference", align_bytes=ALIGN, offset=4 * APART)
+        silu = held.tile([rows, entries], F32, name="silu", align_bytes=ALIGN, offset=5 * APART)
+        product = held.tile([rows, entries], F32, name="product", align_bytes=ALIGN, offset=6 * APART)
 
-        zeros = held.tile([rows, 1], F32, name="zeros")
-        warm = held.tile([rows, 1], F32, name="warm")
+        zeros = held.tile([rows, 1], F32, name="zeros", offset=ALIGN)
+        warm = held.tile([rows, 1], F32, name="warm", offset=2 * ALIGN)
         nc.vector.memset(zeros[:], 0.0)
         nc.scalar.activation(warm[:], zeros[:], SILU)
 

import concourse.mybir as mybir

F32 = mybir.dt.float32
U16 = mybir.dt.uint16
SILU = mybir.ActivationFunctionType.Silu
SUBTRACT = mybir.AluOpType.subtract
MULT = mybir.AluOpType.mult
ALIGN = 4096
APART = 32768
GROUP = 16
LAST = 512
EARLY = 832
FIRST = 512


def tile_lookup_vg_subsilu_out_kernel(tc, tab, y, offs, out):
    nc = tc.nc
    rows, places = tab.shape[1], tab.shape[2]
    entries = y.shape[1]
    middle = EARLY + LAST
    with tc.tile_pool(name="held", bufs=1) as held:
        offsets = held.tile([rows, entries // GROUP], U16, name="offsets", align_bytes=ALIGN, offset=0 * APART)
        values = held.tile([rows, places], F32, name="values", align_bytes=ALIGN, offset=1 * APART)
        gates = held.tile([rows, places], F32, name="gates", align_bytes=ALIGN, offset=2 * APART)
        stream = held.tile([rows, entries], F32, name="stream", align_bytes=ALIGN, offset=3 * APART)
        difference = held.tile([rows, entries], F32, name="difference", align_bytes=ALIGN, offset=4 * APART)
        silu = held.tile([rows, entries], F32, name="silu", align_bytes=ALIGN, offset=5 * APART)
        product = held.tile([rows, entries], F32, name="product", align_bytes=ALIGN, offset=6 * APART)

        zeros = held.tile([rows, 1], F32, name="zeros", offset=ALIGN)
        warm = held.tile([rows, 1], F32, name="warm", offset=2 * ALIGN)
        nc.vector.memset(zeros[:], 0.0)
        nc.scalar.activation(warm[:], zeros[:], SILU)

        nc.sync.dma_start(offsets[:], offs)
        nc.sync.dma_start(values[:], tab[0])
        nc.scalar.dma_start(stream[:, :EARLY], y[:, :EARLY])
        nc.sync.dma_start(gates[:], tab[1])
        nc.sync.dma_start(stream[:, EARLY:middle], y[:, EARLY:middle])
        nc.sync.dma_start(stream[:, middle:], y[:, middle:])

        def subtract(start, stop):
            picks = offsets[:, start // GROUP : stop // GROUP]
            nc.vector.tensor_tensor(difference[:, start:stop], values[:].indirect(picks), stream[:, start:stop], SUBTRACT)

        def multiply(start, stop):
            nc.vector.tensor_tensor(product[:, start:stop], difference[:, start:stop], silu[:, start:stop], MULT)

        def store(start, stop):
            nc.scalar.dma_start(out[:, start:stop], product[:, start:stop])

        for start, stop in ((0, FIRST), (FIRST, entries - LAST), (entries - LAST, entries)):
            nc.scalar.activation(silu[:, start:stop], gates[:].indirect(offsets[:, start // GROUP : stop // GROUP]), SILU)

        subtract(0, EARLY)
        subtract(EARLY, middle)
        multiply(0, FIRST)
        for start in range(0, FIRST, FIRST // 4):
            store(start, start + FIRST // 4)
        subtract(middle, entries)
        for start in range(FIRST, entries, LAST // 2):
            multiply(start, start + LAST // 2)
            store(start, start + LAST // 2)
